import numpy as np
import ml_dtypes


def mxq(x, axis, fmt="e4m3"):
    dtype, down = {"e4m3": (ml_dtypes.float8_e4m3fn, 7), "e5m2": (ml_dtypes.float8_e5m2, 14)}[fmt]
    v = np.moveaxis(np.asarray(x, np.float32).astype(ml_dtypes.bfloat16).astype(np.float64), axis, -1)
    blocks = v.reshape(v.shape[:-1] + (-1, 32))
    amax = np.abs(blocks).max(-1, keepdims=True)
    byte = np.maximum(np.where(amax > 0, np.frexp(amax)[1] - 1 + 127, 0) - down, 1)
    scale = np.exp2(byte - 127.0)
    codes = (blocks / scale).astype(np.float32).astype(dtype).astype(np.float64)
    return np.moveaxis((codes * scale).reshape(v.shape), -1, axis)


WIDE = False


def mx_kscale(k):
    if not WIDE:
        return np.ones(k)
    levels = np.array([10, -10, 5, -5, 0])
    if k % 512:
        return np.exp2(np.random.permutation(np.resize(levels, k // 32))).repeat(32)
    a = np.empty((k // 512, 16))
    for p in range(k // 512):
        a[p, :8] = np.random.permutation(np.resize(levels, 8))
        for g in range(8):
            far = levels[np.abs(levels - a[p, g]) >= 10]
            a[p, g + 8] = far[np.random.randint(len(far))]
    return np.exp2(a.ravel()).repeat(32)


def f64(x):
    return np.asarray(x).astype(np.float64)


def striped(idx):
    return np.tile(np.asarray(idx).reshape(-1, 16).T, (8, 1)).astype(np.uint16)


def unstriped(offs):
    return offs[:16].T.reshape(-1).astype(np.int64)


E2M1 = np.array([0.0, 0.5, 1.0, 1.5, 2.0, 3.0, 4.0, 6.0, -0.0, -0.5, -1.0, -1.5, -2.0, -3.0, -4.0, -6.0])


def pack_weight(w, fmt):
    k, n = w.shape
    w = f64(np.asarray(w, np.float32).astype(ml_dtypes.bfloat16)).reshape(k // 32, 32, n)
    amax = np.abs(w).max(1)
    if fmt == "e4m3":
        byte = np.frexp(amax)[1] - 1 + 127 - 7
    else:
        mant, ex = np.frexp(amax / 6.0)
        byte = np.where(mant > 0.5, ex, ex - 1) + 127
    byte = np.clip(np.where(amax > 0, byte, 1), 1, 254)
    scaled = (w * np.exp2(127.0 - byte)[:, None, :]).reshape(k, n).astype(np.float32)
    by_word = np.ascontiguousarray(scaled.reshape(k // 512, 128, 4, n).transpose(0, 1, 3, 2))
    if fmt == "e4m3":
        words = by_word.astype(ml_dtypes.float8_e4m3fn).view(np.uint8)
    else:
        c = by_word.astype(ml_dtypes.float4_e2m1fn).view(np.uint8) & 0xF
        words = (c[..., 0::2] | (c[..., 1::2] << 4)).reshape(k // 512, 128, 2 * n)
    return np.ascontiguousarray(words), np.ascontiguousarray(byte.astype(np.uint8).reshape(k // 512, 16, n))


def unpack_weight(words, scales, fmt):
    g, _, n = scales.shape
    words = np.ascontiguousarray(words).reshape(g, 128, n, -1)
    if fmt == "e4m3":
        vals = words.view(ml_dtypes.float8_e4m3fn).astype(np.float64)
    else:
        nib = np.empty((g, 128, n, 4), np.uint8)
        nib[..., 0::2] = words & 0xF
        nib[..., 1::2] = words >> 4
        vals = E2M1[nib]
    vals = vals * np.repeat(np.exp2(scales.astype(np.float64) - 127.0), 8, axis=1)[..., None]
    return vals.transpose(0, 1, 3, 2).reshape(g * 512, n)


def softplus(v):
    return np.log(1.0 + np.exp(v))


def sigmoid(v):
    return 1.0 / (1.0 + np.exp(-v))


K, R, F, T, J, M = 512, 128, 512, 2048, 512, 256


def setup_inputs():
    n = np.random.standard_normal
    idx = np.random.permutation(T)[:J]
    idx2 = np.random.permutation(J)[:M]
    idx3 = np.random.permutation(J)[:M]
    fk = mx_kscale(K)
    ff = mx_kscale(F)
    tabp = pack_weight(n((K, T)) / fk[:, None], "e4m3")
    return {
        "tab_words": tabp[0],
        "tab_scales": tabp[1],
        "w1": (n((K, R)) * 1 / np.sqrt(K) * fk[:, None]).astype(np.float32),
        "floor": (np.random.uniform(0.2, 0.8, (R, 1))).astype(np.float32),
        "wo": (n((F, R)) * 1 / np.sqrt(F) * ff[:, None]).astype(np.float32),
        "dy": (n((F, M)) / ff[:, None]).astype(np.float32),
        "old": (0.5 * n((R, J))).astype(np.float32),
        "offs": striped(idx),
        "offs2": striped(idx2),
        "offs3": striped(idx3),
    }


def reference(tab_words, tab_scales, w1, floor, wo, dy, old, offs, offs2, offs3):
    idx = unstriped(offs)
    idx2 = unstriped(offs2)
    idx3 = unstriped(offs3)
    tabu = unpack_weight(tab_words, tab_scales, "e4m3")
    w1q = mxq(f64(w1), 0, "e4m3")
    tabidxg = tabu[:, idx]
    a = w1q.T @ tabidxg
    h0 = softplus(a)
    h1 = np.log(h0 + f64(floor))
    woq = mxq(f64(wo), 0, "e4m3")
    dyq = mxq(f64(dy), 0, "e4m3")
    c0 = woq.T @ dyq
    e1 = c0 * sigmoid(h1[:, idx2])
    s1 = np.zeros((R, J))
    s1[:, idx2] = e1
    e2 = c0 * (h1[:, idx2] - h1[:, idx3]) * sigmoid(h1[:, idx2]) * (1.0 - sigmoid(h1[:, idx2]))
    s2 = np.zeros((R, J))
    s2[:, idx2] = e2
    e3 = c0 * sigmoid(h1[:, idx2]) * (-1.0)
    s3 = np.zeros((R, J))
    s3[:, idx3] = e3
    dh1 = s1 + s2 + s3
    dh0 = dh1 / (h0 + f64(floor))
    da = dh0 * sigmoid(a)
    y = da + f64(old)
    return y

@@ -1,0 +1,176 @@
+from contextlib import ExitStack
+
+import concourse.mybir as mybir
+
+K, R, F, T, J, M = 512, 128, 512, 2048, 512, 256
+FLOPS = 2 * K * R * J + 2 * F * R * M
+
+F32 = mybir.dt.float32
+BF16 = mybir.dt.bfloat16
+I32 = mybir.dt.int32
+U32 = mybir.dt.uint32
+U16 = mybir.dt.uint16
+U8 = mybir.dt.uint8
+FP8X4 = mybir.dt.float8_e4m3fn_x4
+ALU = mybir.AluOpType
+ACT = mybir.ActivationFunctionType
+
+P = 128
+PACK = 4
+LIST_ROWS = 16
+EARLY = T // 4
+HALF = J // 2
+QUARTER = J // 4
+
+
+def quantize(nc, pool, raw, grouped, name):
+    width = raw.shape[2]
+    codes = pool.tile([P, width], U32, align_bytes=64, name=name + "_codes")
+    scales = pool.tile([P, width], U8, align_bytes=64, name=name + "_scales")
+    nc.vector.tensor_copy(
+        out=grouped.rearrange("p (c i) t -> p c t i", i=4),
+        in_=raw[:].rearrange("p t (c i) -> p c t i", i=4),
+    )
+    nc.vector.quantize_mx(out=codes[:].bitcast(FP8X4), scales=scales[:], in_=grouped.rearrange("p w t -> p (w t)"))
+    return codes, scales
+
+
+def tile_attend_clogratios_kernel(tc, tab_words, tab_scales, w1, floor, wo, dy, old, offs, offs2, offs3, out):
+    nc = tc.nc
+    halves = [slice(h * HALF, (h + 1) * HALF) for h in range(2)]
+
+    with ExitStack() as ctx:
+        pool = ctx.enter_context(tc.tile_pool(name="sbuf", bufs=1))
+        psum = ctx.enter_context(tc.psum_pool(name="psum", bufs=1))
+
+        list1 = pool.tile([P, J // LIST_ROWS], U16, name="list1")
+        list2 = pool.tile([P, M // LIST_ROWS], U16, name="list2")
+        list3 = pool.tile([P, M // LIST_ROWS], U16, name="list3")
+        words = pool.tile([P, T], U32, align_bytes=64, tag="table", name="words")
+        scale_bytes = pool.tile([P, T], U8, name="scale_bytes")
+        w1_raw = pool.tile([P, PACK, R], F32, name="w1_raw")
+        wo_raw = pool.tile([P, PACK, R], F32, name="wo_raw")
+        dy_raw = pool.tile([P, PACK, M], F32, name="dy_raw")
+        floor_col = pool.tile([P, 1], F32, name="floor_col")
+        old_sb = pool.tile([P, J], F32, name="old_sb")
+        placed2 = pool.tile([P, J], F32, name="placed2")
+        placed3 = pool.tile([P, J], F32, name="placed3")
+
+        nc.vector.memset(scale_bytes[:].bitcast(I32), 0)
+        nc.sync.dma_start(list1[:], offs)
+        nc.sync.dma_start(out=w1_raw[:], in_=w1.rearrange("(p t) r -> p t r", t=PACK))
+        table_words = tab_words[0].rearrange("p n t -> p (n t)").bitcast(I32)
+        nc.sync.dma_start(out=words[:, :EARLY].bitcast(I32), in_=table_words[:, :EARLY])
+        for i in range(4):
+            nc.sync.dma_start(
+                out=scale_bytes[i:P:32, :].bitcast(I32), in_=tab_scales[0, i:16:4, :].bitcast(I32)
+            )
+        nc.sync.dma_start(out=words[:, EARLY:].bitcast(I32), in_=table_words[:, EARLY:])
+        nc.sync.dma_start(out=wo_raw[:], in_=wo.rearrange("(p t) r -> p t r", t=PACK))
+        nc.sync.dma_start(out=dy_raw[:], in_=dy.rearrange("(p t) m -> p t m", t=PACK))
+        nc.sync.dma_start(out=floor_col[:], in_=floor)
+        nc.sync.dma_start(list2[:], offs2)
+        nc.sync.dma_start(list3[:], offs3)
+        nc.sync.dma_start(out=old_sb[:], in_=old)
+        nc.vector.memset(placed2[:], 0.0)
+        nc.vector.memset(placed3[:], 0.0)
+
+        w1_bf16 = pool.tile([P, R, PACK], BF16, align_bytes=64, name="w1_bf16")
+        w1_codes, w1_scales = quantize(nc, pool, w1_raw, w1_bf16[:], "w1")
+
+        tab_codes = pool.tile([P, J], U32, align_bytes=64, name="tab_codes")
+        tab_bytes = pool.tile([P, J], U8, align_bytes=64, name="tab_bytes")
+        nc.vector.tensor_copy(out=tab_bytes[:], in_=scale_bytes[:].indirect(list1[:]))
+
+        a_ps = [psum.tile([P, HALF], F32, name="a_ps%d" % h) for h in range(2)]
+        mag = pool.tile([P, J], F32, name="mag")
+        decay = pool.tile([P, J], F32, name="decay")
+        for h, cols in enumerate(halves):
+            list_cols = slice(cols.start // LIST_ROWS, cols.stop // LIST_ROWS)
+            nc.vector.tensor_copy(out=tab_codes[:, cols], in_=words[:].indirect(list1[:, list_cols]))
+            nc.tensor.matmul_mx(
+                out=a_ps[h][:],
+                lhsT=w1_codes[:].bitcast(FP8X4),
+                lhsT_scale=w1_scales[:],
+                rhs=tab_codes[:, cols].bitcast(FP8X4),
+                rhs_scale=tab_bytes[:, cols],
+                start=True,
+                stop=True,
+            )
+            nc.scalar.activation(out=mag[:, cols], in_=a_ps[h][:], func=ACT.Abs)
+            nc.scalar.activation(out=decay[:, cols], in_=mag[:, cols], func=ACT.Exp, scale=-1.0)
+
+        last_bf16 = pool.tile([P, R + M, PACK], BF16, align_bytes=64, tag="table", name="last_bf16")
+        wo_codes, wo_scales = quantize(nc, pool, wo_raw, last_bf16[:, :R, :], "wo")
+        dy_codes, dy_scales = quantize(nc, pool, dy_raw, last_bf16[:, R:, :], "dy")
+        c0_ps = psum.tile([P, M], F32, name="c0_ps")
+        nc.tensor.matmul_mx(
+            out=c0_ps[:],
+            lhsT=wo_codes[:].bitcast(FP8X4),
+            lhsT_scale=wo_scales[:],
+            rhs=dy_codes[:].bitcast(FP8X4),
+            rhs_scale=dy_scales[:],
+            start=True,
+            stop=True,
+        )
+        c0 = pool.tile([P, M], F32, name="c0")
+        nc.vector.tensor_copy(out=c0[:], in_=c0_ps[:])
+
+        tail = pool.tile([P, J], F32, name="tail")
+        h0 = pool.tile([P, J], F32, name="h0")
+        h1 = pool.tile([P, J], F32, name="h1")
+        log_slope = pool.tile([P, J], F32, name="log_slope")
+        for q in range(4):
+            cols = slice(q * QUARTER, (q + 1) * QUARTER)
+            a_part = a_ps[q // 2][:, (q % 2) * QUARTER : (q % 2 + 1) * QUARTER]
+            nc.scalar.activation(out=tail[:, cols], in_=decay[:, cols], func=ACT.Ln, bias=1.0)
+            nc.vector.scalar_tensor_tensor(
+                out=h0[:, cols], in0=a_part, scalar=0.0, in1=tail[:, cols], op0=ALU.max, op1=ALU.add
+            )
+        for q in range(4):
+            cols = slice(q * QUARTER, (q + 1) * QUARTER)
+            nc.scalar.activation(out=h1[:, cols], in_=h0[:, cols], func=ACT.Ln, bias=floor_col[:])
+        for h, cols in enumerate(halves):
+            nc.vector.scalar_tensor_tensor(
+                out=log_slope[:, cols], in0=a_ps[h][:], scalar=0.0, in1=tail[:, cols], op0=ALU.min, op1=ALU.subtract
+            )
+
+        first = pool.tile([P, M], F32, name="first")
+        gap = pool.tile([P, M], F32, name="gap")
+        gate = pool.tile([P, M], F32, name="gate")
+        log_factor = pool.tile([P, J], F32, name="log_factor")
+        factor = pool.tile([P, J], F32, name="factor")
+        nc.vector.tensor_copy(out=first[:], in_=h1[:].indirect(list2[:]))
+        nc.scalar.activation(out=gate[:], in_=first[:], func=ACT.Sigmoid)
+        nc.vector.tensor_tensor(out=gap[:], in0=h1[:].indirect(list3[:]), in1=first[:], op=ALU.subtract)
+        nc.vector.tensor_tensor(out=log_factor[:], in0=log_slope[:], in1=h1[:], op=ALU.subtract)
+        nc.scalar.activation(out=factor[:], in_=log_factor[:], func=ACT.Exp)
+
+        bend = pool.tile([P, M], F32, name="bend")
+        weight = pool.tile([P, M], F32, name="weight")
+        nc.vector.scalar_tensor_tensor(
+            out=bend[:], in0=gate[:], scalar=1.0, in1=gap[:], op0=ALU.subtract, op1=ALU.mult
+        )
+        pairs = [slice(h * M // 2, (h + 1) * M // 2) for h in range(2)]
+        pair_cols = [slice(s.start // LIST_ROWS, s.stop // LIST_ROWS) for s in pairs]
+        nc.vector.tensor_tensor(
+            out=placed3[:].indirect(list3[:, pair_cols[0]]), in0=c0[:, pairs[0]], in1=gate[:, pairs[0]], op=ALU.mult
+        )
+        nc.vector.scalar_tensor_tensor(
+            out=weight[:], in0=bend[:], scalar=1.0, in1=gate[:], op0=ALU.add, op1=ALU.mult
+        )
+        nc.vector.tensor_tensor(
+            out=placed3[:].indirect(list3[:, pair_cols[1]]), in0=c0[:, pairs[1]], in1=gate[:, pairs[1]], op=ALU.mult
+        )
+        nc.vector.tensor_tensor(out=placed2[:].indirect(list2[:]), in0=c0[:], in1=weight[:], op=ALU.mult)
+
+        dh1 = pool.tile([P, J], F32, name="dh1")
+        da = pool.tile([P, J], F32, name="da")
+        result = pool.tile([P, J], F32, name="result")
+        for cols in halves:
+            nc.vector.tensor_tensor(out=dh1[:, cols], in0=placed2[:, cols], in1=placed3[:, cols], op=ALU.subtract)
+        for cols in halves:
+            nc.vector.tensor_tensor(out=da[:, cols], in0=dh1[:, cols], in1=factor[:, cols], op=ALU.mult)
+        for cols in halves:
+            nc.vector.tensor_tensor(out=result[:, cols], in0=da[:, cols], in1=old_sb[:, cols], op=ALU.add)
+            nc.sync.dma_start(out=out[:, cols], in_=result[:, cols])

@@ -19,6 +19,7 @@ P = 128
 PACK = 4
 LIST_ROWS = 16
 EARLY = T // 4
+TINY = 2.0**-44
 HALF = J // 2
 QUARTER = J // 4
 
@@ -57,10 +58,10 @@ def tile_attend_clogratios_kernel(tc, tab_words, tab_scales, w1, floor, wo, dy, 
         placed3 = pool.tile([P, J], F32, name="placed3")
 
         nc.vector.memset(scale_bytes[:].bitcast(I32), 0)
-        nc.sync.dma_start(list1[:], offs)
         nc.sync.dma_start(out=w1_raw[:], in_=w1.rearrange("(p t) r -> p t r", t=PACK))
         table_words = tab_words[0].rearrange("p n t -> p (n t)").bitcast(I32)
         nc.sync.dma_start(out=words[:, :EARLY].bitcast(I32), in_=table_words[:, :EARLY])
+        nc.sync.dma_start(list1[:], offs)
         for i in range(4):
             nc.sync.dma_start(
                 out=scale_bytes[i:P:32, :].bitcast(I32), in_=tab_scales[0, i:16:4, :].bitcast(I32)
@@ -83,7 +84,6 @@ def tile_attend_clogratios_kernel(tc, tab_words, tab_scales, w1, floor, wo, dy, 
         nc.vector.tensor_copy(out=tab_bytes[:], in_=scale_bytes[:].indirect(list1[:]))
 
         a_ps = [psum.tile([P, HALF], F32, name="a_ps%d" % h) for h in range(2)]
-        mag = pool.tile([P, J], F32, name="mag")
         decay = pool.tile([P, J], F32, name="decay")
         for h, cols in enumerate(halves):
             list_cols = slice(cols.start // LIST_ROWS, cols.stop // LIST_ROWS)
@@ -97,8 +97,7 @@ def tile_attend_clogratios_kernel(tc, tab_words, tab_scales, w1, floor, wo, dy, 
                 start=True,
                 stop=True,
             )
-            nc.scalar.activation(out=mag[:, cols], in_=a_ps[h][:], func=ACT.Abs)
-            nc.scalar.activation(out=decay[:, cols], in_=mag[:, cols], func=ACT.Exp, scale=-1.0)
+            nc.scalar.activation(out=decay[:, cols], in_=a_ps[h][:], func=ACT.Sigmoid, scale=-1.0)
 
         last_bf16 = pool.tile([P, R + M, PACK], BF16, align_bytes=64, tag="table", name="last_bf16")
         wo_codes, wo_scales = quantize(nc, pool, wo_raw, last_bf16[:, :R, :], "wo")
@@ -123,27 +122,27 @@ def tile_attend_clogratios_kernel(tc, tab_words, tab_scales, w1, floor, wo, dy, 
         for q in range(4):
             cols = slice(q * QUARTER, (q + 1) * QUARTER)
             a_part = a_ps[q // 2][:, (q % 2) * QUARTER : (q % 2 + 1) * QUARTER]
-            nc.scalar.activation(out=tail[:, cols], in_=decay[:, cols], func=ACT.Ln, bias=1.0)
+            nc.scalar.activation(out=tail[:, cols], in_=decay[:, cols], func=ACT.Ln, bias=TINY)
             nc.vector.scalar_tensor_tensor(
-                out=h0[:, cols], in0=a_part, scalar=0.0, in1=tail[:, cols], op0=ALU.max, op1=ALU.add
+                out=h0[:, cols], in0=tail[:, cols], scalar=-1.0, in1=a_part, op0=ALU.mult, op1=ALU.max
             )
         for q in range(4):
             cols = slice(q * QUARTER, (q + 1) * QUARTER)
             nc.scalar.activation(out=h1[:, cols], in_=h0[:, cols], func=ACT.Ln, bias=floor_col[:])
         for h, cols in enumerate(halves):
-            nc.vector.scalar_tensor_tensor(
-                out=log_slope[:, cols], in0=a_ps[h][:], scalar=0.0, in1=tail[:, cols], op0=ALU.min, op1=ALU.subtract
-            )
+            nc.vector.tensor_tensor(out=log_slope[:, cols], in0=a_ps[h][:], in1=h0[:, cols], op=ALU.subtract)
 
         first = pool.tile([P, M], F32, name="first")
         gap = pool.tile([P, M], F32, name="gap")
         gate = pool.tile([P, M], F32, name="gate")
         log_factor = pool.tile([P, J], F32, name="log_factor")
         factor = pool.tile([P, J], F32, name="factor")
+        left, right = halves
+        nc.vector.tensor_tensor(out=log_factor[:, left], in0=log_slope[:, left], in1=h1[:, left], op=ALU.subtract)
         nc.vector.tensor_copy(out=first[:], in_=h1[:].indirect(list2[:]))
+        nc.vector.tensor_tensor(out=log_factor[:, right], in0=log_slope[:, right], in1=h1[:, right], op=ALU.subtract)
         nc.scalar.activation(out=gate[:], in_=first[:], func=ACT.Sigmoid)
         nc.vector.tensor_tensor(out=gap[:], in0=h1[:].indirect(list3[:]), in1=first[:], op=ALU.subtract)
-        nc.vector.tensor_tensor(out=log_factor[:], in0=log_slope[:], in1=h1[:], op=ALU.subtract)
         nc.scalar.activation(out=factor[:], in_=log_factor[:], func=ACT.Exp)
 
         bend = pool.tile([P, M], F32, name="bend")

@@ -1,6 +1,7 @@
 from contextlib import ExitStack
 
 import concourse.mybir as mybir
+from concourse.masks import make_identity
 
 K, R, F, T, J, M = 512, 128, 512, 2048, 512, 256
 FLOPS = 2 * K * R * J + 2 * F * R * M
@@ -76,6 +77,8 @@ def tile_attend_clogratios_kernel(tc, tab_words, tab_scales, w1, floor, wo, dy, 
         nc.vector.memset(placed2[:], 0.0)
         nc.vector.memset(placed3[:], 0.0)
 
+        identity = pool.tile([P, P], F32, name="identity")
+        make_identity(nc, identity[:])
         w1_bf16 = pool.tile([P, R, PACK], BF16, align_bytes=64, name="w1_bf16")
         w1_codes, w1_scales = quantize(nc, pool, w1_raw, w1_bf16[:], "w1")
 
@@ -130,20 +133,27 @@ def tile_attend_clogratios_kernel(tc, tab_words, tab_scales, w1, floor, wo, dy, 
             cols = slice(q * QUARTER, (q + 1) * QUARTER)
             nc.scalar.activation(out=h1[:, cols], in_=h0[:, cols], func=ACT.Ln, bias=floor_col[:])
         for h, cols in enumerate(halves):
-            nc.vector.tensor_tensor(out=log_slope[:, cols], in0=a_ps[h][:], in1=h0[:, cols], op=ALU.subtract)
+            nc.vector.tensor_tensor(out=log_slope[:, cols], in0=h0[:, cols], in1=a_ps[h][:], op=ALU.subtract)
 
         first = pool.tile([P, M], F32, name="first")
         gap = pool.tile([P, M], F32, name="gap")
         gate = pool.tile([P, M], F32, name="gate")
-        log_factor = pool.tile([P, J], F32, name="log_factor")
-        factor = pool.tile([P, J], F32, name="factor")
-        left, right = halves
-        nc.vector.tensor_tensor(out=log_factor[:, left], in0=log_slope[:, left], in1=h1[:, left], op=ALU.subtract)
+        log_factor = psum.tile([P, J], F32, name="log_factor")
+        factor_t = pool.tile([P, J], F32, name="factor_t")
+        factor = psum.tile([P, J], F32, name="factor")
         nc.vector.tensor_copy(out=first[:], in_=h1[:].indirect(list2[:]))
-        nc.vector.tensor_tensor(out=log_factor[:, right], in0=log_slope[:, right], in1=h1[:, right], op=ALU.subtract)
         nc.scalar.activation(out=gate[:], in_=first[:], func=ACT.Sigmoid)
         nc.vector.tensor_tensor(out=gap[:], in0=h1[:].indirect(list3[:]), in1=first[:], op=ALU.subtract)
-        nc.scalar.activation(out=factor[:], in_=log_factor[:], func=ACT.Exp)
+        for q in range(4):
+            cols = slice(q * P, (q + 1) * P)
+            for term, opens in ((log_slope, True), (h1, False)):
+                nc.tensor.matmul(
+                    log_factor[:, cols], lhsT=term[:, cols], rhs=identity[:], is_transpose=True, start=opens, stop=not opens
+                )
+        nc.scalar.activation(out=factor_t[:], in_=log_factor[:], func=ACT.Exp, scale=-1.0)
+        for q in range(4):
+            cols = slice(q * P, (q + 1) * P)
+            nc.tensor.transpose(factor[:, cols], factor_t[:, cols], identity[:])
 
         bend = pool.tile([P, M], F32, name="bend")
         weight = pool.tile([P, M], F32, name="weight")

from contextlib import ExitStack

import concourse.mybir as mybir
from concourse.masks import make_identity

K, R, F, T, J, M = 512, 128, 512, 2048, 512, 256
FLOPS = 2 * K * R * J + 2 * F * R * M

F32 = mybir.dt.float32
BF16 = mybir.dt.bfloat16
I32 = mybir.dt.int32
U32 = mybir.dt.uint32
U16 = mybir.dt.uint16
U8 = mybir.dt.uint8
FP8X4 = mybir.dt.float8_e4m3fn_x4
ALU = mybir.AluOpType
ACT = mybir.ActivationFunctionType

P = 128
PACK = 4
LIST_ROWS = 16
EARLY = T // 4
TINY = 2.0**-44
HALF = J // 2
QUARTER = J // 4


def quantize(nc, pool, raw, grouped, name):
    width = raw.shape[2]
    codes = pool.tile([P, width], U32, align_bytes=64, name=name + "_codes")
    scales = pool.tile([P, width], U8, align_bytes=64, name=name + "_scales")
    nc.vector.tensor_copy(
        out=grouped.rearrange("p (c i) t -> p c t i", i=4),
        in_=raw[:].rearrange("p t (c i) -> p c t i", i=4),
    )
    nc.vector.quantize_mx(out=codes[:].bitcast(FP8X4), scales=scales[:], in_=grouped.rearrange("p w t -> p (w t)"))
    return codes, scales


def tile_attend_clogratios_kernel(tc, tab_words, tab_scales, w1, floor, wo, dy, old, offs, offs2, offs3, out):
    nc = tc.nc
    halves = [slice(h * HALF, (h + 1) * HALF) for h in range(2)]

    with ExitStack() as ctx:
        pool = ctx.enter_context(tc.tile_pool(name="sbuf", bufs=1))
        psum = ctx.enter_context(tc.psum_pool(name="psum", bufs=1))

        list1 = pool.tile([P, J // LIST_ROWS], U16, name="list1")
        list2 = pool.tile([P, M // LIST_ROWS], U16, name="list2")
        list3 = pool.tile([P, M // LIST_ROWS], U16, name="list3")
        words = pool.tile([P, T], U32, align_bytes=64, tag="table", name="words")
        scale_bytes = pool.tile([P, T], U8, name="scale_bytes")
        w1_raw = pool.tile([P, PACK, R], F32, name="w1_raw")
        wo_raw = pool.tile([P, PACK, R], F32, name="wo_raw")
        dy_raw = pool.tile([P, PACK, M], F32, name="dy_raw")
        floor_col = pool.tile([P, 1], F32, name="floor_col")
        old_sb = pool.tile([P, J], F32, name="old_sb")
        placed2 = pool.tile([P, J], F32, name="placed2")
        placed3 = pool.tile([P, J], F32, name="placed3")

        nc.vector.memset(scale_bytes[:].bitcast(I32), 0)
        nc.sync.dma_start(out=w1_raw[:], in_=w1.rearrange("(p t) r -> p t r", t=PACK))
        table_words = tab_words[0].rearrange("p n t -> p (n t)").bitcast(I32)
        nc.sync.dma_start(out=words[:, :EARLY].bitcast(I32), in_=table_words[:, :EARLY])
        nc.sync.dma_start(list1[:], offs)
        for i in range(4):
            nc.sync.dma_start(
                out=scale_bytes[i:P:32, :].bitcast(I32), in_=tab_scales[0, i:16:4, :].bitcast(I32)
            )
        nc.sync.dma_start(out=words[:, EARLY:].bitcast(I32), in_=table_words[:, EARLY:])
        nc.sync.dma_start(out=wo_raw[:], in_=wo.rearrange("(p t) r -> p t r", t=PACK))
        nc.sync.dma_start(out=dy_raw[:], in_=dy.rearrange("(p t) m -> p t m", t=PACK))
        nc.sync.dma_start(out=floor_col[:], in_=floor)
        nc.sync.dma_start(list2[:], offs2)
        nc.sync.dma_start(list3[:], offs3)
        nc.sync.dma_start(out=old_sb[:], in_=old)
        nc.vector.memset(placed2[:], 0.0)
        nc.vector.memset(placed3[:], 0.0)

        identity = pool.tile([P, P], F32, name="identity")
        make_identity(nc, identity[:])
        w1_bf16 = pool.tile([P, R, PACK], BF16, align_bytes=64, name="w1_bf16")
        w1_codes, w1_scales = quantize(nc, pool, w1_raw, w1_bf16[:], "w1")

        tab_codes = pool.tile([P, J], U32, align_bytes=64, name="tab_codes")
        tab_bytes = pool.tile([P, J], U8, align_bytes=64, name="tab_bytes")
        nc.vector.tensor_copy(out=tab_bytes[:], in_=scale_bytes[:].indirect(list1[:]))

        a_ps = [psum.tile([P, HALF], F32, name="a_ps%d" % h) for h in range(2)]
        decay = pool.tile([P, J], F32, name="decay")
        for h, cols in enumerate(halves):
            list_cols = slice(cols.start // LIST_ROWS, cols.stop // LIST_ROWS)
            nc.vector.tensor_copy(out=tab_codes[:, cols], in_=words[:].indirect(list1[:, list_cols]))
            nc.tensor.matmul_mx(
                out=a_ps[h][:],
                lhsT=w1_codes[:].bitcast(FP8X4),
                lhsT_scale=w1_scales[:],
                rhs=tab_codes[:, cols].bitcast(FP8X4),
                rhs_scale=tab_bytes[:, cols],
                start=True,
                stop=True,
            )
            nc.scalar.activation(out=decay[:, cols], in_=a_ps[h][:], func=ACT.Sigmoid, scale=-1.0)

        last_bf16 = pool.tile([P, R + M, PACK], BF16, align_bytes=64, tag="table", name="last_bf16")
        wo_codes, wo_scales = quantize(nc, pool, wo_raw, last_bf16[:, :R, :], "wo")
        dy_codes, dy_scales = quantize(nc, pool, dy_raw, last_bf16[:, R:, :], "dy")
        c0_ps = psum.tile([P, M], F32, name="c0_ps")
        nc.tensor.matmul_mx(
            out=c0_ps[:],
            lhsT=wo_codes[:].bitcast(FP8X4),
            lhsT_scale=wo_scales[:],
            rhs=dy_codes[:].bitcast(FP8X4),
            rhs_scale=dy_scales[:],
            start=True,
            stop=True,
        )
        c0 = pool.tile([P, M], F32, name="c0")
        nc.vector.tensor_copy(out=c0[:], in_=c0_ps[:])

        tail = pool.tile([P, J], F32, name="tail")
        h0 = pool.tile([P, J], F32, name="h0")
        h1 = pool.tile([P, J], F32, name="h1")
        log_slope = pool.tile([P, J], F32, name="log_slope")
        for q in range(4):
            cols = slice(q * QUARTER, (q + 1) * QUARTER)
            a_part = a_ps[q // 2][:, (q % 2) * QUARTER : (q % 2 + 1) * QUARTER]
            nc.scalar.activation(out=tail[:, cols], in_=decay[:, cols], func=ACT.Ln, bias=TINY)
            nc.vector.scalar_tensor_tensor(
                out=h0[:, cols], in0=tail[:, cols], scalar=-1.0, in1=a_part, op0=ALU.mult, op1=ALU.max
            )
        for q in range(4):
            cols = slice(q * QUARTER, (q + 1) * QUARTER)
            nc.scalar.activation(out=h1[:, cols], in_=h0[:, cols], func=ACT.Ln, bias=floor_col[:])
        for h, cols in enumerate(halves):
            nc.vector.tensor_tensor(out=log_slope[:, cols], in0=h0[:, cols], in1=a_ps[h][:], op=ALU.subtract)

        first = pool.tile([P, M], F32, name="first")
        gap = pool.tile([P, M], F32, name="gap")
        gate = pool.tile([P, M], F32, name="gate")
        log_factor = psum.tile([P, J], F32, name="log_factor")
        factor_t = pool.tile([P, J], F32, name="factor_t")
        factor = psum.tile([P, J], F32, name="factor")
        nc.vector.tensor_copy(out=first[:], in_=h1[:].indirect(list2[:]))
        nc.scalar.activation(out=gate[:], in_=first[:], func=ACT.Sigmoid)
        nc.vector.tensor_tensor(out=gap[:], in0=h1[:].indirect(list3[:]), in1=first[:], op=ALU.subtract)
        for q in range(4):
            cols = slice(q * P, (q + 1) * P)
            for term, opens in ((log_slope, True), (h1, False)):
                nc.tensor.matmul(
                    log_factor[:, cols], lhsT=term[:, cols], rhs=identity[:], is_transpose=True, start=opens, stop=not opens
                )
        nc.scalar.activation(out=factor_t[:], in_=log_factor[:], func=ACT.Exp, scale=-1.0)
        for q in range(4):
            cols = slice(q * P, (q + 1) * P)
            nc.tensor.transpose(factor[:, cols], factor_t[:, cols], identity[:])

        bend = pool.tile([P, M], F32, name="bend")
        weight = pool.tile([P, M], F32, name="weight")
        nc.vector.scalar_tensor_tensor(
            out=bend[:], in0=gate[:], scalar=1.0, in1=gap[:], op0=ALU.subtract, op1=ALU.mult
        )
        pairs = [slice(h * M // 2, (h + 1) * M // 2) for h in range(2)]
        pair_cols = [slice(s.start // LIST_ROWS, s.stop // LIST_ROWS) for s in pairs]
        nc.vector.tensor_tensor(
            out=placed3[:].indirect(list3[:, pair_cols[0]]), in0=c0[:, pairs[0]], in1=gate[:, pairs[0]], op=ALU.mult
        )
        nc.vector.scalar_tensor_tensor(
            out=weight[:], in0=bend[:], scalar=1.0, in1=gate[:], op0=ALU.add, op1=ALU.mult
        )
        nc.vector.tensor_tensor(
            out=placed3[:].indirect(list3[:, pair_cols[1]]), in0=c0[:, pairs[1]], in1=gate[:, pairs[1]], op=ALU.mult
        )
        nc.vector.tensor_tensor(out=placed2[:].indirect(list2[:]), in0=c0[:], in1=weight[:], op=ALU.mult)

        dh1 = pool.tile([P, J], F32, name="dh1")
        da = pool.tile([P, J], F32, name="da")
        result = pool.tile([P, J], F32, name="result")
        for cols in halves:
            nc.vector.tensor_tensor(out=dh1[:, cols], in0=placed2[:, cols], in1=placed3[:, cols], op=ALU.subtract)
        for cols in halves:
            nc.vector.tensor_tensor(out=da[:, cols], in0=dh1[:, cols], in1=factor[:, cols], op=ALU.mult)
        for cols in halves:
            nc.vector.tensor_tensor(out=result[:, cols], in0=da[:, cols], in1=old_sb[:, cols], op=ALU.add)
            nc.sync.dma_start(out=out[:, cols], in_=result[:, cols])
